import numpy as np
import ml_dtypes


def mxq(x, axis, fmt="e4m3"):
    dtype, down = {"e4m3": (ml_dtypes.float8_e4m3fn, 7), "e5m2": (ml_dtypes.float8_e5m2, 14)}[fmt]
    v = np.moveaxis(np.asarray(x, np.float32).astype(ml_dtypes.bfloat16).astype(np.float64), axis, -1)
    blocks = v.reshape(v.shape[:-1] + (-1, 32))
    amax = np.abs(blocks).max(-1, keepdims=True)
    byte = np.maximum(np.where(amax > 0, np.frexp(amax)[1] - 1 + 127, 0) - down, 1)
    scale = np.exp2(byte - 127.0)
    codes = (blocks / scale).astype(np.float32).astype(dtype).astype(np.float64)
    return np.moveaxis((codes * scale).reshape(v.shape), -1, axis)


WIDE = False


def mx_kscale(k):
    if not WIDE:
        return np.ones(k)
    levels = np.array([10, -10, 5, -5, 0])
    if k % 512:
        return np.exp2(np.random.permutation(np.resize(levels, k // 32))).repeat(32)
    a = np.empty((k // 512, 16))
    for p in range(k // 512):
        a[p, :8] = np.random.permutation(np.resize(levels, 8))
        for g in range(8):
            far = levels[np.abs(levels - a[p, g]) >= 10]
            a[p, g + 8] = far[np.random.randint(len(far))]
    return np.exp2(a.ravel()).repeat(32)


def f64(x):
    return np.asarray(x).astype(np.float64)


def striped(idx):
    return np.tile(idx.reshape(-1, 16).T, (8, 1)).astype(np.uint16)


def unstriped(offs):
    return offs[:16].T.reshape(-1).astype(np.int64)


def pack_weight(w):
    k, n = w.shape
    w = f64(np.asarray(w, np.float32).astype(ml_dtypes.bfloat16)).reshape(k // 32, 32, n)
    amax = np.abs(w).max(1)
    byte = np.clip(np.where(amax > 0, np.frexp(amax)[1] - 1 + 127 - 7, 1), 1, 254)
    scaled = (w * np.exp2(127.0 - byte)[:, None, :]).reshape(k, n).astype(np.float32)
    words = np.ascontiguousarray(scaled.reshape(k // 512, 128, 4, n).transpose(0, 1, 3, 2)).astype(ml_dtypes.float8_e4m3fn).view(np.uint8)
    return words, np.ascontiguousarray(byte.astype(np.uint8).reshape(k // 512, 16, n))


def unpack_weight(words, scales):
    g, p, n, _ = words.shape
    vals = np.ascontiguousarray(words).view(ml_dtypes.float8_e4m3fn).astype(np.float64) * np.repeat(np.exp2(scales.astype(np.float64) - 127.0), 8, axis=1)[..., None]
    return vals.transpose(0, 1, 3, 2).reshape(g * 512, n)


def planes(y):
    n, m = y.shape
    v = y.astype(np.float32).astype(ml_dtypes.bfloat16).astype(np.float64).reshape(n // 32, 32, m)
    top = np.abs(v).max(1)
    byte = np.clip(np.where(top > 0, np.frexp(top)[1] - 1 + 127 - 7, 1), 1, 254)
    codes = (v * np.exp2(127.0 - byte)[:, None, :]).reshape(n, m).astype(np.float32).astype(ml_dtypes.float8_e4m3fn).view(np.uint8)
    words = codes.reshape(n // 512, 128, 4, m).transpose(0, 1, 3, 2)
    return np.ascontiguousarray(words), np.ascontiguousarray(byte.astype(np.uint8).reshape(n // 512, 16, m))


def sigmoid(v):
    return 1.0 / (1.0 + np.exp(-np.maximum(v, -700.0)))


K, T, S, H, J, N, U = 512, 1024, 512, 512, 512, 512, 1024
P = 2 ** 7


def setup_inputs():
    n = np.random.standard_normal
    s = mx_kscale(K)[:, None]
    u = mx_kscale(H)
    packed_xT = pack_weight(n((K, T)) * s)
    return {
        "x_words": packed_xT[0],
        "x_scales": packed_xT[1],
        "mem": (n((H, U)) * u[:, None]).astype(np.float32),
        "wd": (n((H, J)) / np.sqrt(H) / u[:, None]).astype(np.float32),
        "w1": (n((K, N)) / np.sqrt(K) / s).astype(np.float32),
        "w2": (n((K, N)) / np.sqrt(K) / s).astype(np.float32),
        "w3": (n((K, N)) / np.sqrt(K) / s).astype(np.float32),
        "unit": (np.random.uniform(0.6, 1.4, (H, 1)) / u[:, None]).astype(np.float32),
        "fade": (np.tile(np.random.uniform(0.1, 1.0, S), (P, 1))).astype(np.float32),
        "offs": striped(np.random.permutation(T)[:S]),
        "slot": striped(np.random.permutation(U)[:S]),
    }


def reference(x_words, x_scales, mem, wd, w1, w2, w3, unit, fade, offs, slot):
    xq = unpack_weight(x_words, x_scales)[:, unstriped(offs)]
    f = sigmoid(mxq(f64(w1), 0, "e4m3").T @ xq)
    old = f64(mem)[:, unstriped(slot)]
    ov = f64(unit) * old
    cs = np.tanh(mxq(f64(wd), 0, "e4m3").T @ mxq(old, 0, "e4m3"))
    adj = ov - cs + cs * f64(fade)[:1]
    a = sigmoid(mxq(f64(w2), 0, "e4m3").T @ xq)
    out_0 = f * adj + a * (np.tanh(mxq(f64(w3), 0, "e4m3").T @ xq))
    return (out_0,) + planes(out_0)

@@ -1,0 +1,254 @@
+from contextlib import ExitStack
+
+import concourse.mybir as mybir
+from concourse.masks import make_identity
+
+K, T, S, U, N = 512, 1024, 512, 1024, 512
+FLOPS = 4 * 2 * K * N * S
+
+F32 = mybir.dt.float32
+BF16 = mybir.dt.bfloat16
+I32 = mybir.dt.int32
+U32 = mybir.dt.uint32
+U16 = mybir.dt.uint16
+U8 = mybir.dt.uint8
+FP8X4 = mybir.dt.float8_e4m3fn_x4
+ALU = mybir.AluOpType
+ACT = mybir.ActivationFunctionType
+
+P = 128
+PACK = 4
+CHUNKS = S // P
+HALF = N // 2
+QUADS = 4
+
+
+def tile_picked_ytlstm_cell_po_kernel(
+    tc, x_words, x_scales, mem, wd, w1, w2, w3, unit, fade, offs, slot, out_0, out_1, out_2
+):
+    nc = tc.nc
+    with ExitStack() as ctx:
+        keep = ctx.enter_context(tc.tile_pool(name="keep", bufs=1))
+        psum_mm = ctx.enter_context(tc.psum_pool(name="psum_mm", bufs=4))
+        psum_tr = ctx.enter_context(tc.psum_pool(name="psum_tr", bufs=4))
+
+        def sb(name, shape, dtype):
+            return keep.tile(shape, dtype, name=name, align_bytes=64)
+
+        offs_t = keep.tile([P, S // 16], U16, name="offs_t")
+        slot_t = keep.tile([P, S // 16], U16, name="slot_t")
+        x_table = sb("x_table", [P, T], I32)
+        xs_table = sb("xs_table", [P, T], U8)
+        mem_t = [sb(f"mem{t}", [P, U], F32) for t in range(PACK)]
+        weights = {"w1": w1, "w2": w2, "w3": w3, "wd": wd}
+        raw = {(w, h): sb(f"raw_{w}{h}", [P, PACK, HALF], F32) for w in weights for h in range(2)}
+        unit_t = sb("unit_t", [P, PACK], F32)
+        fade_rows = sb("fade_rows", [P, P], F32)
+        ident = sb("ident", [P, P], F32)
+
+        def load_w(w, h):
+            view = weights[w].rearrange("(p j) n -> p j n", j=PACK)
+            nc.sync.dma_start(out=raw[w, h][:], in_=view[:, :, h * HALF : (h + 1) * HALF])
+
+        def load_mem(t):
+            nc.sync.dma_start(out=mem_t[t][:], in_=mem.rearrange("(p t) u -> p t u", t=PACK)[:, t, :])
+
+        nc.vector.memset(xs_table[:].bitcast(I32), 0)
+        nc.sync.dma_start(out=x_table[:], in_=x_words[0].rearrange("p n t -> p (n t)").bitcast(I32))
+        for q in range(QUADS):
+            nc.sync.dma_start(
+                out=xs_table[32 * q : 32 * q + 4, :].bitcast(I32),
+                in_=x_scales[0, 4 * q : 4 * q + 4, :].bitcast(I32),
+            )
+        nc.sync.dma_start(offs_t[:], offs)
+        load_w("w1", 0)
+        nc.sync.dma_start(slot_t[:], slot)
+        load_mem(0)
+        load_w("w1", 1)
+        load_mem(1)
+        load_w("w2", 0)
+        load_mem(2)
+        load_w("w2", 1)
+        load_mem(3)
+        load_w("w3", 0)
+        load_w("w3", 1)
+        load_w("wd", 0)
+        load_w("wd", 1)
+        nc.gpsimd.dma_start(out=fade_rows[:], in_=fade.rearrange("r (c m) -> (r c) m", m=P)[0:P, :])
+        nc.gpsimd.dma_start(out=unit_t[:], in_=unit.rearrange("(p t) o -> p (t o)", t=PACK))
+        make_identity(nc, ident[:])
+
+        def interleave(engine, dst, src):
+            d = dst.rearrange("p (c i) t -> p c t i", i=4)
+            s = src.rearrange("p t (c i) -> p c t i", i=4)
+            if engine == "scalar":
+                nc.scalar.copy(out=d, in_=s)
+            else:
+                nc.vector.tensor_copy(out=d, in_=s)
+
+        def quantize(codes, scales, grouped):
+            nc.vector.quantize_mx(out=codes.bitcast(FP8X4), scales=scales, in_=grouped.rearrange("p c t -> p (c t)"))
+
+        grouped = {}
+        codes = {}
+        scales = {}
+
+        def cast_w(w, h, engine):
+            grouped[w, h] = sb(f"grp_{w}{h}", [P, HALF, PACK], BF16)
+            interleave(engine, grouped[w, h][:], raw[w, h][:])
+
+        def quant_w(w, h):
+            codes[w, h] = sb(f"codes_{w}{h}", [P, HALF], U32)
+            scales[w, h] = sb(f"scales_{w}{h}", [P, HALF], U8)
+            quantize(codes[w, h][:], scales[w, h][:], grouped[w, h][:])
+
+        gates = {(w, pr): sb(f"gate_{w}{pr}", [P, 2, PACK, P], F32) for w in weights for pr in range(2)}
+
+        def product(w, h, lhs_codes, lhs_scales, func):
+            for pr in range(2):
+                bank = psum_mm.tile([P, 2, HALF], F32, name="bank")
+                for i in range(2):
+                    cols = slice((2 * pr + i) * P, (2 * pr + i + 1) * P)
+                    nc.tensor.matmul_mx(
+                        out=bank[:, i, :],
+                        lhsT=lhs_codes[:, cols].bitcast(FP8X4),
+                        lhsT_scale=lhs_scales[:, cols],
+                        rhs=codes[w, h][:].bitcast(FP8X4),
+                        rhs_scale=scales[w, h][:],
+                        start=True,
+                        stop=True,
+                    )
+                nc.scalar.activation(
+                    out=gates[w, pr][:, :, :, h * 64 : (h + 1) * 64],
+                    in_=bank[:].rearrange("p c (m t) -> p c t m", t=PACK),
+                    func=func,
+                )
+
+        x_codes = sb("x_codes", [P, S], U32)
+        x_sc = sb("x_sc", [P, S], U8)
+        old = sb("old", [P, PACK, S], F32)
+
+        def gather_mem(t):
+            nc.vector.tensor_copy(old[:, t, :], mem_t[t][:].indirect(slot_t[:]))
+
+        nc.vector.tensor_copy(x_codes[:], x_table[:].bitcast(U32).indirect(offs_t[:]))
+        nc.vector.tensor_copy(x_sc[:], xs_table[:].indirect(offs_t[:]))
+        cast_w("w1", 0, "scalar")
+        gather_mem(0)
+        quant_w("w1", 0)
+        product("w1", 0, x_codes, x_sc, ACT.Sigmoid)
+        cast_w("w1", 1, "scalar")
+        gather_mem(1)
+        quant_w("w1", 1)
+        product("w1", 1, x_codes, x_sc, ACT.Sigmoid)
+
+        fade_ps = psum_mm.tile([P, 2, HALF], F32, name="bank")
+        nc.tensor.transpose(fade_ps[:, 0, 0:P], fade_rows[:], ident[:])
+        fade_m1 = sb("fade_m1", [P, CHUNKS], F32)
+        nc.vector.tensor_scalar_add(fade_m1[:], fade_ps[:, 0, 0:CHUNKS], -1.0)
+
+        f_banks = []
+        for t in range(PACK):
+            fb = psum_tr.tile([P, PACK, P], F32, name="turned")
+            for c in range(CHUNKS):
+                nc.tensor.transpose(fb[:, c, :], gates["w1", c // 2][:, c % 2, t, :], ident[:])
+            f_banks.append(fb)
+
+        kept = sb("kept", [P, PACK, S], F32)
+
+        def keep_term(t):
+            nc.vector.scalar_tensor_tensor(
+                out=kept[:, t, :],
+                in0=old[:, t, :],
+                scalar=unit_t[:, t : t + 1],
+                in1=f_banks[t][:].rearrange("p c m -> p (c m)"),
+                op0=ALU.mult,
+                op1=ALU.mult,
+            )
+
+        cast_w("w2", 0, "scalar")
+        gather_mem(2)
+        quant_w("w2", 0)
+        product("w2", 0, x_codes, x_sc, ACT.Sigmoid)
+        cast_w("w2", 1, "scalar")
+        keep_term(0)
+        keep_term(1)
+        gather_mem(3)
+        quant_w("w2", 1)
+        product("w2", 1, x_codes, x_sc, ACT.Sigmoid)
+
+        old_grouped = sb("old_grouped", [P, S, PACK], BF16)
+        interleave("vector", old_grouped[:], old[:])
+        cast_w("w3", 0, "scalar")
+        keep_term(2)
+        old_codes = sb("old_codes", [P, S], U32)
+        old_scales = sb("old_scales", [P, S], U8)
+        quantize(old_codes[:], old_scales[:], old_grouped[:])
+        keep_term(3)
+        quant_w("w3", 0)
+        product("w3", 0, x_codes, x_sc, ACT.Tanh)
+        cast_w("w3", 1, "scalar")
+        cast_w("wd", 0, "vector")
+        quant_w("w3", 1)
+        product("w3", 1, x_codes, x_sc, ACT.Tanh)
+        quant_w("wd", 0)
+        cast_w("wd", 1, "vector")
+        product("wd", 0, old_codes, old_scales, ACT.Tanh)
+        new = [sb(f"new{pr}", [P, 2, PACK, P], F32) for pr in range(2)]
+        nc.vector.tensor_tensor(out=new[0][:], in0=gates["w2", 0][:], in1=gates["w3", 0][:], op=ALU.mult)
+        quant_w("wd", 1)
+        product("wd", 1, old_codes, old_scales, ACT.Tanh)
+        nc.vector.tensor_tensor(out=new[1][:], in0=gates["w2", 1][:], in1=gates["w3", 1][:], op=ALU.mult)
+
+        y_codes = sb("y_codes", [P, S], U32)
+        y_scales = sb("y_scales", [P, S], U8)
+        out_rows = out_0.rearrange("(p t) n -> p t n", t=PACK)
+        out_words = out_1[0].rearrange("p n t -> p (n t)").bitcast(I32)
+        sums = {}
+        y_grouped = {}
+
+        def lost_term(c):
+            lost = sb(f"lost{c}", [P, PACK, P], F32)
+            nc.vector.scalar_tensor_tensor(
+                out=lost[:],
+                in0=gates["wd", c // 2][:, c % 2, :, :],
+                scalar=fade_m1[:, c : c + 1],
+                in1=gates["w1", c // 2][:, c % 2, :, :],
+                op0=ALU.mult,
+                op1=ALU.mult,
+            )
+            sums[c] = psum_tr.tile([P, PACK, P], F32, name="turned")
+            for t in range(PACK):
+                nc.tensor.matmul(
+                    sums[c][:, t, :], lhsT=new[c // 2][:, c % 2, t, :], rhs=ident[:], is_transpose=True, start=True, stop=False
+                )
+                nc.tensor.matmul(
+                    sums[c][:, t, :], lhsT=lost[:, t, :], rhs=ident[:], is_transpose=True, start=False, stop=True
+                )
+
+        def result(c):
+            cols = slice(c * P, (c + 1) * P)
+            y = sb(f"y{c}", [P, PACK, P], F32)
+            nc.vector.tensor_tensor(out=y[:], in0=kept[:, :, cols], in1=sums[c][:], op=ALU.add)
+            nc.sync.dma_start(out=out_rows[:, :, cols], in_=y[:])
+            y_grouped[c] = sb(f"y_grouped{c}", [P, P, PACK], BF16)
+            interleave("scalar", y_grouped[c][:], y[:])
+
+        def planes(c):
+            cols = slice(c * P, (c + 1) * P)
+            quantize(y_codes[:, cols], y_scales[:, cols], y_grouped[c][:])
+            nc.sync.dma_start(out=out_words[:, cols], in_=y_codes[:, cols].bitcast(I32))
+
+        for step in range(CHUNKS + 2):
+            if step < CHUNKS:
+                lost_term(step)
+            if 1 <= step <= CHUNKS:
+                result(step - 1)
+            if step >= 2:
+                planes(step - 2)
+        for q in range(QUADS):
+            queue = nc.sync if q % 2 == 0 else nc.scalar
+            queue.dma_start(
+                out=out_2[0, 4 * q : 4 * q + 4, :].bitcast(I32),
+                in_=y_scales[32 * q : 32 * q + 4, :].bitcast(I32),
+            )

@@ -32,28 +32,28 @@ def tile_picked_ytlstm_cell_po_kernel(
         psum_mm = ctx.enter_context(tc.psum_pool(name="psum_mm", bufs=4))
         psum_tr = ctx.enter_context(tc.psum_pool(name="psum_tr", bufs=4))
 
-        def sb(name, shape, dtype):
-            return keep.tile(shape, dtype, name=name, align_bytes=64)
+        def sb(name, shape, dtype, tag=""):
+            return keep.tile(shape, dtype, name=name, tag=tag, align_bytes=64)
 
         offs_t = keep.tile([P, S // 16], U16, name="offs_t")
         slot_t = keep.tile([P, S // 16], U16, name="slot_t")
         x_table = sb("x_table", [P, T], I32)
         xs_table = sb("xs_table", [P, T], U8)
-        mem_t = [sb(f"mem{t}", [P, U], F32) for t in range(PACK)]
+        mem_t = [sb(f"mem{t}", [P, U], F32, tag=f"mem{t}") for t in range(PACK)]
         weights = {"w1": w1, "w2": w2, "w3": w3, "wd": wd}
-        raw = {(w, h): sb(f"raw_{w}{h}", [P, PACK, HALF], F32) for w in weights for h in range(2)}
+        raw = {(w, h): sb(f"raw_{w}{h}", [P, PACK, HALF], F32)[:] for w in weights for h in range(2)}
         unit_t = sb("unit_t", [P, PACK], F32)
         fade_rows = sb("fade_rows", [P, P], F32)
         ident = sb("ident", [P, P], F32)
 
         def load_w(w, h):
             view = weights[w].rearrange("(p j) n -> p j n", j=PACK)
-            nc.sync.dma_start(out=raw[w, h][:], in_=view[:, :, h * HALF : (h + 1) * HALF])
+            nc.sync.dma_start(out=raw[w, h], in_=view[:, :, h * HALF : (h + 1) * HALF])
 
         def load_mem(t):
             nc.sync.dma_start(out=mem_t[t][:], in_=mem.rearrange("(p t) u -> p t u", t=PACK)[:, t, :])
 
-        nc.vector.memset(xs_table[:].bitcast(I32), 0)
+        nc.gpsimd.memset(xs_table[:].bitcast(I32), 0)
         nc.sync.dma_start(out=x_table[:], in_=x_words[0].rearrange("p n t -> p (n t)").bitcast(I32))
         for q in range(QUADS):
             nc.sync.dma_start(
@@ -62,11 +62,13 @@ def tile_picked_ytlstm_cell_po_kernel(
             )
         nc.sync.dma_start(offs_t[:], offs)
         load_w("w1", 0)
+        load_w("w1", 1)
+        load_w("w2", 0)
         nc.sync.dma_start(slot_t[:], slot)
         load_mem(0)
-        load_w("w1", 1)
         load_mem(1)
-        load_w("w2", 0)
+        nc.sync.dma_start(out=unit_t[:], in_=unit.rearrange("(p t) o -> p (t o)", t=PACK))
+        nc.sync.dma_start(out=fade_rows[:], in_=fade.rearrange("r (c m) -> (r c) m", m=P)[0:P, :])
         load_mem(2)
         load_w("w2", 1)
         load_mem(3)
@@ -74,9 +76,10 @@ def tile_picked_ytlstm_cell_po_kernel(
         load_w("w3", 1)
         load_w("wd", 0)
         load_w("wd", 1)
-        nc.gpsimd.dma_start(out=fade_rows[:], in_=fade.rearrange("r (c m) -> (r c) m", m=P)[0:P, :])
-        nc.gpsimd.dma_start(out=unit_t[:], in_=unit.rearrange("(p t) o -> p (t o)", t=PACK))
         make_identity(nc, ident[:])
+        warm = sb("warm", [P, 2], F32)
+        nc.vector.memset(warm[:, 0:1], 0.0)
+        nc.scalar.activation(out=warm[:, 1:2], in_=warm[:, 0:1], func=ACT.Sigmoid)
 
         def interleave(engine, dst, src):
             d = dst.rearrange("p (c i) t -> p c t i", i=4)
@@ -95,7 +98,7 @@ def tile_picked_ytlstm_cell_po_kernel(
 
         def cast_w(w, h, engine):
             grouped[w, h] = sb(f"grp_{w}{h}", [P, HALF, PACK], BF16)
-            interleave(engine, grouped[w, h][:], raw[w, h][:])
+            interleave(engine, grouped[w, h][:], raw[w, h])
 
         def quant_w(w, h):
             codes[w, h] = sb(f"codes_{w}{h}", [P, HALF], U32)
@@ -133,28 +136,25 @@ def tile_picked_ytlstm_cell_po_kernel(
 
         nc.vector.tensor_copy(x_codes[:], x_table[:].bitcast(U32).indirect(offs_t[:]))
         nc.vector.tensor_copy(x_sc[:], xs_table[:].indirect(offs_t[:]))
-        cast_w("w1", 0, "scalar")
-        gather_mem(0)
-        quant_w("w1", 0)
-        product("w1", 0, x_codes, x_sc, ACT.Sigmoid)
-        cast_w("w1", 1, "scalar")
-        gather_mem(1)
-        quant_w("w1", 1)
-        product("w1", 1, x_codes, x_sc, ACT.Sigmoid)
-
-        fade_ps = psum_mm.tile([P, 2, HALF], F32, name="bank")
-        nc.tensor.transpose(fade_ps[:, 0, 0:P], fade_rows[:], ident[:])
         fade_m1 = sb("fade_m1", [P, CHUNKS], F32)
-        nc.vector.tensor_scalar_add(fade_m1[:], fade_ps[:, 0, 0:CHUNKS], -1.0)
+        f_banks = {}
+        kept = sb("kept", [P, PACK, S], F32, tag="mem3")
+        old_grouped = sb("old_grouped", [P, S, PACK], BF16)
+        old_codes = sb("old_codes", [P, S], U32)
+        old_scales = sb("old_scales", [P, S], U8)
+        new = [sb(f"new{pr}", [P, 2, PACK, P], F32) for pr in range(2)]
+        lost = [sb(f"lost{c}", [P, PACK, P], F32) for c in range(CHUNKS)]
+        sums = {}
 
-        f_banks = []
-        for t in range(PACK):
-            fb = psum_tr.tile([P, PACK, P], F32, name="turned")
+        def fade_column():
+            fade_ps = psum_mm.tile([P, 2, HALF], F32, name="bank")
+            nc.tensor.transpose(fade_ps[:, 0, 0:P], fade_rows[:], ident[:])
+            nc.vector.tensor_scalar_add(fade_m1[:], fade_ps[:, 0, 0:CHUNKS], -1.0)
+
+        def turn_f(t):
+            f_banks[t] = psum_tr.tile([P, PACK, P], F32, name="turned")
             for c in range(CHUNKS):
-                nc.tensor.transpose(fb[:, c, :], gates["w1", c // 2][:, c % 2, t, :], ident[:])
-            f_banks.append(fb)
-
-        kept = sb("kept", [P, PACK, S], F32)
+                nc.tensor.transpose(f_banks[t][:, c, :], gates["w1", c // 2][:, c % 2, t, :], ident[:])
 
         def keep_term(t):
             nc.vector.scalar_tensor_tensor(
@@ -166,64 +166,88 @@ def tile_picked_ytlstm_cell_po_kernel(
                 op1=ALU.mult,
             )
 
+        def cast_old(h, engine):
+            cols = slice(h * HALF, (h + 1) * HALF)
+            interleave(engine, old_grouped[:, cols, :], old[:, :, cols])
+
+        def new_term(pr, engine):
+            engine.tensor_tensor(out=new[pr][:], in0=gates["w2", pr][:], in1=gates["w3", pr][:], op=ALU.mult)
+            for c in (2 * pr, 2 * pr + 1):
+                sums[c] = psum_tr.tile([P, PACK, P], F32, name="turned")
+                for t in range(PACK):
+                    nc.tensor.matmul(
+                        sums[c][:, t, :], lhsT=new[pr][:, c % 2, t, :], rhs=ident[:], is_transpose=True, start=(t == 0), stop=False
+                    )
+
+        def lost_half(c, h):
+            cols = slice(h * 64, (h + 1) * 64)
+            nc.vector.scalar_tensor_tensor(
+                out=lost[c][:, :, cols],
+                in0=gates["wd", c // 2][:, c % 2, :, cols],
+                scalar=fade_m1[:, c : c + 1],
+                in1=gates["w1", c // 2][:, c % 2, :, cols],
+                op0=ALU.mult,
+                op1=ALU.mult,
+            )
+
+        cast_w("w1", 0, "scalar")
+        cast_w("w1", 1, "vector")
+        quant_w("w1", 0)
+        quant_w("w1", 1)
         cast_w("w2", 0, "scalar")
-        gather_mem(2)
+        product("w1", 0, x_codes, x_sc, ACT.Sigmoid)
+        product("w1", 1, x_codes, x_sc, ACT.Sigmoid)
+        gather_mem(0)
         quant_w("w2", 0)
-        product("w2", 0, x_codes, x_sc, ACT.Sigmoid)
+        gather_mem(1)
         cast_w("w2", 1, "scalar")
+        product("w2", 0, x_codes, x_sc, ACT.Sigmoid)
+        turn_f(0)
+        turn_f(1)
+        turn_f(2)
+        turn_f(3)
+        fade_column()
         keep_term(0)
+        quant_w("w2", 1)
+        gather_mem(2)
+        product("w2", 1, x_codes, x_sc, ACT.Sigmoid)
         keep_term(1)
         gather_mem(3)
-        quant_w("w2", 1)
-        product("w2", 1, x_codes, x_sc, ACT.Sigmoid)
-
-        old_grouped = sb("old_grouped", [P, S, PACK], BF16)
-        interleave("vector", old_grouped[:], old[:])
-        cast_w("w3", 0, "scalar")
-        keep_term(2)
-        old_codes = sb("old_codes", [P, S], U32)
-        old_scales = sb("old_scales", [P, S], U8)
-        quantize(old_codes[:], old_scales[:], old_grouped[:])
-        keep_term(3)
+        cast_old(0, "scalar")
+        cast_old(1, "scalar")
+        cast_w("w3", 0, "vector")
         quant_w("w3", 0)
-        product("w3", 0, x_codes, x_sc, ACT.Tanh)
-        cast_w("w3", 1, "scalar")
-        cast_w("wd", 0, "vector")
+        cast_w("w3", 1, "vector")
         quant_w("w3", 1)
+        product("w3", 0, x_codes, x_sc, ACT.Tanh)
         product("w3", 1, x_codes, x_sc, ACT.Tanh)
+        cast_w("wd", 0, "scalar")
         quant_w("wd", 0)
+        quantize(old_codes[:], old_scales[:], old_grouped[:])
         cast_w("wd", 1, "vector")
-        product("wd", 0, old_codes, old_scales, ACT.Tanh)
-        new = [sb(f"new{pr}", [P, 2, PACK, P], F32) for pr in range(2)]
-        nc.vector.tensor_tensor(out=new[0][:], in0=gates["w2", 0][:], in1=gates["w3", 0][:], op=ALU.mult)
         quant_w("wd", 1)
+        product("wd", 0, old_codes, old_scales, ACT.Tanh)
         product("wd", 1, old_codes, old_scales, ACT.Tanh)
-        nc.vector.tensor_tensor(out=new[1][:], in0=gates["w2", 1][:], in1=gates["w3", 1][:], op=ALU.mult)
+        keep_term(2)
+        keep_term(3)
+        new_term(0, nc.vector)
+        new_term(1, nc.vector)
+        lost_half(0, 0)
+        lost_half(1, 0)
+        lost_half(2, 0)
+        lost_half(3, 0)
 
         y_codes = sb("y_codes", [P, S], U32)
         y_scales = sb("y_scales", [P, S], U8)
         out_rows = out_0.rearrange("(p t) n -> p t n", t=PACK)
         out_words = out_1[0].rearrange("p n t -> p (n t)").bitcast(I32)
-        sums = {}
         y_grouped = {}
 
         def lost_term(c):
-            lost = sb(f"lost{c}", [P, PACK, P], F32)
-            nc.vector.scalar_tensor_tensor(
-                out=lost[:],
-                in0=gates["wd", c // 2][:, c % 2, :, :],
-                scalar=fade_m1[:, c : c + 1],
-                in1=gates["w1", c // 2][:, c % 2, :, :],
-                op0=ALU.mult,
-                op1=ALU.mult,
-            )
-            sums[c] = psum_tr.tile([P, PACK, P], F32, name="turned")
+            lost_half(c, 1)
             for t in range(PACK):
                 nc.tensor.matmul(
-                    sums[c][:, t, :], lhsT=new[c // 2][:, c % 2, t, :], rhs=ident[:], is_transpose=True, start=True, stop=False
-                )
-                nc.tensor.matmul(
-                    sums[c][:, t, :], lhsT=lost[:, t, :], rhs=ident[:], is_transpose=True, start=False, stop=True
+                    sums[c][:, t, :], lhsT=lost[c][:, t, :], rhs=ident[:], is_transpose=True, start=False, stop=(t == PACK - 1)
                 )
 
         def result(c):
@@ -232,12 +256,14 @@ def tile_picked_ytlstm_cell_po_kernel(
             nc.vector.tensor_tensor(out=y[:], in0=kept[:, :, cols], in1=sums[c][:], op=ALU.add)
             nc.sync.dma_start(out=out_rows[:, :, cols], in_=y[:])
             y_grouped[c] = sb(f"y_grouped{c}", [P, P, PACK], BF16)
-            interleave("scalar", y_grouped[c][:], y[:])
+            interleave("scalar" if c < CHUNKS - 1 else "vector", y_grouped[c][:], y[:])
 
         def planes(c):
             cols = slice(c * P, (c + 1) * P)
             quantize(y_codes[:, cols], y_scales[:, cols], y_grouped[c][:])
-            nc.sync.dma_start(out=out_words[:, cols], in_=y_codes[:, cols].bitcast(I32))
+            if c % 2 == 1:
+                done = slice((c - 1) * P, (c + 1) * P)
+                nc.sync.dma_start(out=out_words[:, done], in_=y_codes[:, done].bitcast(I32))
 
         for step in range(CHUNKS + 2):
             if step < CHUNKS:

@@ -29,8 +29,9 @@ def tile_picked_ytlstm_cell_po_kernel(
     nc = tc.nc
     with ExitStack() as ctx:
         keep = ctx.enter_context(tc.tile_pool(name="keep", bufs=1))
-        psum_mm = ctx.enter_context(tc.psum_pool(name="psum_mm", bufs=4))
-        psum_tr = ctx.enter_context(tc.psum_pool(name="psum_tr", bufs=4))
+        psum = ctx.enter_context(tc.psum_pool(name="psum", bufs=1))
+
+        banks = [psum.tile([P, N], F32, name=f"bank{b}") for b in range(8)]
 
         def sb(name, shape, dtype, tag=""):
             return keep.tile(shape, dtype, name=name, tag=tag, align_bytes=64)
@@ -41,14 +42,15 @@ def tile_picked_ytlstm_cell_po_kernel(
         xs_table = sb("xs_table", [P, T], U8)
         mem_t = [sb(f"mem{t}", [P, U], F32, tag=f"mem{t}") for t in range(PACK)]
         weights = {"w1": w1, "w2": w2, "w3": w3, "wd": wd}
-        raw = {(w, h): sb(f"raw_{w}{h}", [P, PACK, HALF], F32)[:] for w in weights for h in range(2)}
+        raw = {w: sb(f"raw_{w}", [P, PACK, N], F32, tag=f"raw_{w}") for w in ("w1", "w2", "wd")}
+        raw["old"] = sb("old", [P, PACK, S], F32)
+        old = raw["old"]
         unit_t = sb("unit_t", [P, PACK], F32)
         fade_rows = sb("fade_rows", [P, P], F32)
         ident = sb("ident", [P, P], F32)
 
-        def load_w(w, h):
-            view = weights[w].rearrange("(p j) n -> p j n", j=PACK)
-            nc.sync.dma_start(out=raw[w, h], in_=view[:, :, h * HALF : (h + 1) * HALF])
+        def load_weight(w):
+            nc.sync.dma_start(out=raw[w][:], in_=weights[w].rearrange("(p j) n -> p j n", j=PACK))
 
         def load_mem(t):
             nc.sync.dma_start(out=mem_t[t][:], in_=mem.rearrange("(p t) u -> p t u", t=PACK)[:, t, :])
@@ -61,21 +63,21 @@ def tile_picked_ytlstm_cell_po_kernel(
                 in_=x_scales[0, 4 * q : 4 * q + 4, :].bitcast(I32),
             )
         nc.sync.dma_start(offs_t[:], offs)
-        load_w("w1", 0)
-        load_w("w1", 1)
-        load_w("w2", 0)
+        nc.sync.dma_start(out=fade_rows[:], in_=fade.rearrange("r (c m) -> (r c) m", m=P)[0:P, :])
+        load_weight("w1")
         nc.sync.dma_start(slot_t[:], slot)
+        load_weight("w2")
         load_mem(0)
         load_mem(1)
-        nc.sync.dma_start(out=unit_t[:], in_=unit.rearrange("(p t) o -> p (t o)", t=PACK))
-        nc.sync.dma_start(out=fade_rows[:], in_=fade.rearrange("r (c m) -> (r c) m", m=P)[0:P, :])
         load_mem(2)
-        load_w("w2", 1)
         load_mem(3)
-        load_w("w3", 0)
-        load_w("w3", 1)
-        load_w("wd", 0)
-        load_w("wd", 1)
+        nc.sync.dma_start(out=unit_t[:], in_=unit.rearrange("(p t) o -> p (t o)", t=PACK))
+        w3_view = w3.rearrange("(p j) n -> p j n", j=PACK)
+        raw_w3a = sb("raw_w3a", [P, PACK, 256], F32, tag="raw_w3a")
+        raw_w3b = sb("raw_w3b", [P, PACK, N - 256], F32)
+        nc.sync.dma_start(out=raw_w3a[:], in_=w3_view[:, :, 0:256])
+        nc.sync.dma_start(out=raw_w3b[:], in_=w3_view[:, :, 256:N])
+        load_weight("wd")
         make_identity(nc, ident[:])
         warm = sb("warm", [P, 2], F32)
         nc.vector.memset(warm[:, 0:1], 0.0)
@@ -86,77 +88,68 @@ def tile_picked_ytlstm_cell_po_kernel(
             s = src.rearrange("p t (c i) -> p c t i", i=4)
             if engine == "scalar":
                 nc.scalar.copy(out=d, in_=s)
+            elif engine == "gpsimd":
+                nc.gpsimd.tensor_scalar(out=d, in0=s, scalar1=1.0, scalar2=0.0, op0=ALU.mult, op1=ALU.add)
             else:
                 nc.vector.tensor_copy(out=d, in_=s)
 
-        def quantize(codes, scales, grouped):
-            nc.vector.quantize_mx(out=codes.bitcast(FP8X4), scales=scales, in_=grouped.rearrange("p c t -> p (c t)"))
+        def quantize(codes_ap, scales_ap, grouped_ap):
+            nc.vector.quantize_mx(
+                out=codes_ap.bitcast(FP8X4), scales=scales_ap, in_=grouped_ap.rearrange("p c t -> p (c t)")
+            )
 
-        grouped = {}
-        codes = {}
-        scales = {}
+        kept = sb("kept", [P, PACK, S], F32)
+        grouped = {w: sb(f"grp_{w}", [P, N, PACK], BF16) for w in weights}
+        grouped["old"] = sb("grp_old", [P, S, PACK], BF16, tag="raw_w3a")
+        codes = {name: sb(f"codes_{name}", [P, N], U32) for name in list(weights) + ["old", "x"]}
+        scales = {name: sb(f"scales_{name}", [P, N], U8) for name in list(weights) + ["old", "x"]}
 
-        def cast_w(w, h, engine):
-            grouped[w, h] = sb(f"grp_{w}{h}", [P, HALF, PACK], BF16)
-            interleave(engine, grouped[w, h][:], raw[w, h])
+        def round_columns(name, first, last, engine):
+            cols = slice(first, last)
+            interleave(engine, grouped[name][:, cols, :], raw[name][:, :, cols])
 
-        def quant_w(w, h):
-            codes[w, h] = sb(f"codes_{w}{h}", [P, HALF], U32)
-            scales[w, h] = sb(f"scales_{w}{h}", [P, HALF], U8)
-            quantize(codes[w, h][:], scales[w, h][:], grouped[w, h][:])
+        def quantize_operand(name):
+            quantize(codes[name][:], scales[name][:], grouped[name][:])
 
-        gates = {(w, pr): sb(f"gate_{w}{pr}", [P, 2, PACK, P], F32) for w in weights for pr in range(2)}
+        partner = {"w1": "x", "w2": "x", "w3": "x", "wd": "old"}
+        func = {"w1": ACT.Sigmoid, "w2": ACT.Sigmoid, "w3": ACT.Tanh, "wd": ACT.Tanh}
+        first_bank = {"w1": 0, "w2": 4, "w3": 0, "wd": 4}
+        gate_tiles = {w: sb(f"gate_{w}", [P, CHUNKS, PACK, P], F32, tag="" if w == "w1" else "") for w in weights}
+        gates = {(w, c): gate_tiles[w][:, c] for w in weights for c in range(CHUNKS)}
 
-        def product(w, h, lhs_codes, lhs_scales, func):
-            for pr in range(2):
-                bank = psum_mm.tile([P, 2, HALF], F32, name="bank")
-                for i in range(2):
-                    cols = slice((2 * pr + i) * P, (2 * pr + i + 1) * P)
-                    nc.tensor.matmul_mx(
-                        out=bank[:, i, :],
-                        lhsT=lhs_codes[:, cols].bitcast(FP8X4),
-                        lhsT_scale=lhs_scales[:, cols],
-                        rhs=codes[w, h][:].bitcast(FP8X4),
-                        rhs_scale=scales[w, h][:],
-                        start=True,
-                        stop=True,
-                    )
-                nc.scalar.activation(
-                    out=gates[w, pr][:, :, :, h * 64 : (h + 1) * 64],
-                    in_=bank[:].rearrange("p c (m t) -> p c t m", t=PACK),
-                    func=func,
-                )
-
-        x_codes = sb("x_codes", [P, S], U32)
-        x_sc = sb("x_sc", [P, S], U8)
-        old = sb("old", [P, PACK, S], F32)
+        def gate(w, c):
+            cols = slice(c * P, (c + 1) * P)
+            bank = banks[first_bank[w] + c]
+            nc.tensor.matmul_mx(
+                out=bank[:],
+                lhsT=codes[partner[w]][:, cols].bitcast(FP8X4),
+                lhsT_scale=scales[partner[w]][:, cols],
+                rhs=codes[w][:].bitcast(FP8X4),
+                rhs_scale=scales[w][:],
+                start=True,
+                stop=True,
+            )
+            nc.scalar.activation(out=gates[w, c][:], in_=bank[:].rearrange("p (m t) -> p t m", t=PACK), func=func[w])
 
         def gather_mem(t):
             nc.vector.tensor_copy(old[:, t, :], mem_t[t][:].indirect(slot_t[:]))
 
-        nc.vector.tensor_copy(x_codes[:], x_table[:].bitcast(U32).indirect(offs_t[:]))
-        nc.vector.tensor_copy(x_sc[:], xs_table[:].indirect(offs_t[:]))
         fade_m1 = sb("fade_m1", [P, CHUNKS], F32)
         f_banks = {}
-        kept = sb("kept", [P, PACK, S], F32, tag="mem3")
-        old_grouped = sb("old_grouped", [P, S, PACK], BF16)
-        old_codes = sb("old_codes", [P, S], U32)
-        old_scales = sb("old_scales", [P, S], U8)
-        new = [sb(f"new{pr}", [P, 2, PACK, P], F32) for pr in range(2)]
-        lost = [sb(f"lost{c}", [P, PACK, P], F32) for c in range(CHUNKS)]
         sums = {}
+        new_all = sb("new", [P, CHUNKS, PACK, P], F32, tag="raw_wd")
 
         def fade_column():
-            fade_ps = psum_mm.tile([P, 2, HALF], F32, name="bank")
-            nc.tensor.transpose(fade_ps[:, 0, 0:P], fade_rows[:], ident[:])
-            nc.vector.tensor_scalar_add(fade_m1[:], fade_ps[:, 0, 0:CHUNKS], -1.0)
+            fade_ps = banks[4]
+            nc.tensor.transpose(fade_ps[:, 0:P], fade_rows[:], ident[:])
+            nc.vector.tensor_scalar_add(fade_m1[:], fade_ps[:, 0:CHUNKS], -1.0)
 
-        def turn_f(t):
-            f_banks[t] = psum_tr.tile([P, PACK, P], F32, name="turned")
+        def turn_forget(t):
+            f_banks[t] = banks[4 + t][:].rearrange("p (c m) -> p c m", c=CHUNKS)
             for c in range(CHUNKS):
-                nc.tensor.transpose(f_banks[t][:, c, :], gates["w1", c // 2][:, c % 2, t, :], ident[:])
+                nc.tensor.transpose(f_banks[t][:, c, :], gates["w1", c][:, t, :], ident[:])
 
-        def keep_term(t):
+        def kept_term(t):
             nc.vector.scalar_tensor_tensor(
                 out=kept[:, t, :],
                 in0=old[:, t, :],
@@ -166,76 +159,29 @@ def tile_picked_ytlstm_cell_po_kernel(
                 op1=ALU.mult,
             )
 
-        def cast_old(h, engine):
-            cols = slice(h * HALF, (h + 1) * HALF)
-            interleave(engine, old_grouped[:, cols, :], old[:, :, cols])
+        def new_term(c, engine):
+            new = new_all[:, c]
+            engine.tensor_tensor(out=new[:], in0=gates["w2", c][:], in1=gates["w3", c][:], op=ALU.mult)
+            sums[c] = banks[0 + c][:].rearrange("p (t m) -> p t m", t=PACK)
+            for t in range(PACK):
+                nc.tensor.matmul(
+                    sums[c][:, t, :], lhsT=new[:, t, :], rhs=ident[:], is_transpose=True, start=(t == 0), stop=False
+                )
 
-        def new_term(pr, engine):
-            engine.tensor_tensor(out=new[pr][:], in0=gates["w2", pr][:], in1=gates["w3", pr][:], op=ALU.mult)
-            for c in (2 * pr, 2 * pr + 1):
-                sums[c] = psum_tr.tile([P, PACK, P], F32, name="turned")
-                for t in range(PACK):
-                    nc.tensor.matmul(
-                        sums[c][:, t, :], lhsT=new[pr][:, c % 2, t, :], rhs=ident[:], is_transpose=True, start=(t == 0), stop=False
-                    )
-
-        def lost_half(c, h):
-            cols = slice(h * 64, (h + 1) * 64)
+        def lost_term(c):
+            lost = sb(f"lost{c}", [P, PACK, P], F32)
             nc.vector.scalar_tensor_tensor(
-                out=lost[c][:, :, cols],
-                in0=gates["wd", c // 2][:, c % 2, :, cols],
+                out=lost[:],
+                in0=gates["wd", c][:],
                 scalar=fade_m1[:, c : c + 1],
-                in1=gates["w1", c // 2][:, c % 2, :, cols],
+                in1=gates["w1", c][:],
                 op0=ALU.mult,
                 op1=ALU.mult,
             )
-
-        cast_w("w1", 0, "scalar")
-        cast_w("w1", 1, "vector")
-        quant_w("w1", 0)
-        quant_w("w1", 1)
-        cast_w("w2", 0, "scalar")
-        product("w1", 0, x_codes, x_sc, ACT.Sigmoid)
-        product("w1", 1, x_codes, x_sc, ACT.Sigmoid)
-        gather_mem(0)
-        quant_w("w2", 0)
-        gather_mem(1)
-        cast_w("w2", 1, "scalar")
-        product("w2", 0, x_codes, x_sc, ACT.Sigmoid)
-        turn_f(0)
-        turn_f(1)
-        turn_f(2)
-        turn_f(3)
-        fade_column()
-        keep_term(0)
-        quant_w("w2", 1)
-        gather_mem(2)
-        product("w2", 1, x_codes, x_sc, ACT.Sigmoid)
-        keep_term(1)
-        gather_mem(3)
-        cast_old(0, "scalar")
-        cast_old(1, "scalar")
-        cast_w("w3", 0, "vector")
-        quant_w("w3", 0)
-        cast_w("w3", 1, "vector")
-        quant_w("w3", 1)
-        product("w3", 0, x_codes, x_sc, ACT.Tanh)
-        product("w3", 1, x_codes, x_sc, ACT.Tanh)
-        cast_w("wd", 0, "scalar")
-        quant_w("wd", 0)
-        quantize(old_codes[:], old_scales[:], old_grouped[:])
-        cast_w("wd", 1, "vector")
-        quant_w("wd", 1)
-        product("wd", 0, old_codes, old_scales, ACT.Tanh)
-        product("wd", 1, old_codes, old_scales, ACT.Tanh)
-        keep_term(2)
-        keep_term(3)
-        new_term(0, nc.vector)
-        new_term(1, nc.vector)
-        lost_half(0, 0)
-        lost_half(1, 0)
-        lost_half(2, 0)
-        lost_half(3, 0)
+            for t in range(PACK):
+                nc.tensor.matmul(
+                    sums[c][:, t, :], lhsT=lost[:, t, :], rhs=ident[:], is_transpose=True, start=False, stop=(t == PACK - 1)
+                )
 
         y_codes = sb("y_codes", [P, S], U32)
         y_scales = sb("y_scales", [P, S], U8)
@@ -243,20 +189,13 @@ def tile_picked_ytlstm_cell_po_kernel(
         out_words = out_1[0].rearrange("p n t -> p (n t)").bitcast(I32)
         y_grouped = {}
 
-        def lost_term(c):
-            lost_half(c, 1)
-            for t in range(PACK):
-                nc.tensor.matmul(
-                    sums[c][:, t, :], lhsT=lost[c][:, t, :], rhs=ident[:], is_transpose=True, start=False, stop=(t == PACK - 1)
-                )
-
-        def result(c):
+        def result(c, engine):
             cols = slice(c * P, (c + 1) * P)
             y = sb(f"y{c}", [P, PACK, P], F32)
             nc.vector.tensor_tensor(out=y[:], in0=kept[:, :, cols], in1=sums[c][:], op=ALU.add)
             nc.sync.dma_start(out=out_rows[:, :, cols], in_=y[:])
             y_grouped[c] = sb(f"y_grouped{c}", [P, P, PACK], BF16)
-            interleave("scalar" if c < CHUNKS - 1 else "vector", y_grouped[c][:], y[:])
+            interleave(engine, y_grouped[c][:], y[:])
 
         def planes(c):
             cols = slice(c * P, (c + 1) * P)
@@ -265,13 +204,67 @@ def tile_picked_ytlstm_cell_po_kernel(
                 done = slice((c - 1) * P, (c + 1) * P)
                 nc.sync.dma_start(out=out_words[:, done], in_=y_codes[:, done].bitcast(I32))
 
-        for step in range(CHUNKS + 2):
-            if step < CHUNKS:
-                lost_term(step)
-            if 1 <= step <= CHUNKS:
-                result(step - 1)
-            if step >= 2:
-                planes(step - 2)
+        nc.vector.tensor_copy(codes["x"][:], x_table[:].bitcast(U32).indirect(offs_t[:]))
+        nc.vector.tensor_copy(scales["x"][:], xs_table[:].indirect(offs_t[:]))
+        fade_column()
+        round_columns("w1", 0, 192, "scalar")
+        round_columns("w1", 192, 512, "vector")
+        quantize_operand("w1")
+        round_columns("w2", 0, 512, "vector")
+        quantize_operand("w2")
+        gate("w1", 0)
+        gate("w1", 1)
+        gate("w1", 2)
+        gate("w1", 3)
+        gather_mem(0)
+        gather_mem(1)
+        gate("w2", 0)
+        gate("w2", 1)
+        gate("w2", 2)
+        gate("w2", 3)
+        turn_forget(0)
+        turn_forget(1)
+        turn_forget(2)
+        turn_forget(3)
+        gather_mem(2)
+        gather_mem(3)
+        interleave("scalar", grouped["w3"][:, 0:256, :], raw_w3a[:])
+        interleave("scalar", grouped["w3"][:, 256:N, :], raw_w3b[:])
+        round_columns("old", 0, 256, "scalar")
+        round_columns("old", 256, 512, "scalar")
+        quantize_operand("w3")
+        round_columns("wd", 0, 128, "scalar")
+        round_columns("wd", 128, 512, "vector")
+        quantize_operand("wd")
+        quantize_operand("old")
+        kept_term(0)
+        kept_term(1)
+        kept_term(2)
+        kept_term(3)
+        gate("w3", 0)
+        gate("w3", 1)
+        gate("w3", 2)
+        gate("w3", 3)
+        gate("wd", 0)
+        gate("wd", 1)
+        gate("wd", 2)
+        gate("wd", 3)
+        new_term(0, nc.vector)
+        new_term(1, nc.vector)
+        new_term(2, nc.vector)
+        new_term(3, nc.vector)
+        lost_term(0)
+        lost_term(1)
+        lost_term(2)
+        result(0, "scalar")
+        lost_term(3)
+        result(1, "scalar")
+        planes(0)
+        result(2, "scalar")
+        planes(1)
+        result(3, "vector")
+        planes(2)
+        planes(3)
         for q in range(QUADS):
             queue = nc.sync if q % 2 == 0 else nc.scalar
             queue.dma_start(

from contextlib import ExitStack

import concourse.mybir as mybir
from concourse.masks import make_identity

K, T, S, U, N = 512, 1024, 512, 1024, 512
FLOPS = 4 * 2 * K * N * S

F32 = mybir.dt.float32
BF16 = mybir.dt.bfloat16
I32 = mybir.dt.int32
U32 = mybir.dt.uint32
U16 = mybir.dt.uint16
U8 = mybir.dt.uint8
FP8X4 = mybir.dt.float8_e4m3fn_x4
ALU = mybir.AluOpType
ACT = mybir.ActivationFunctionType

P = 128
PACK = 4
CHUNKS = S // P
HALF = N // 2
QUADS = 4


def tile_picked_ytlstm_cell_po_kernel(
    tc, x_words, x_scales, mem, wd, w1, w2, w3, unit, fade, offs, slot, out_0, out_1, out_2
):
    nc = tc.nc
    with ExitStack() as ctx:
        keep = ctx.enter_context(tc.tile_pool(name="keep", bufs=1))
        psum = ctx.enter_context(tc.psum_pool(name="psum", bufs=1))

        banks = [psum.tile([P, N], F32, name=f"bank{b}") for b in range(8)]

        def sb(name, shape, dtype, tag=""):
            return keep.tile(shape, dtype, name=name, tag=tag, align_bytes=64)

        offs_t = keep.tile([P, S // 16], U16, name="offs_t")
        slot_t = keep.tile([P, S // 16], U16, name="slot_t")
        x_table = sb("x_table", [P, T], I32)
        xs_table = sb("xs_table", [P, T], U8)
        mem_t = [sb(f"mem{t}", [P, U], F32, tag=f"mem{t}") for t in range(PACK)]
        weights = {"w1": w1, "w2": w2, "w3": w3, "wd": wd}
        raw = {w: sb(f"raw_{w}", [P, PACK, N], F32, tag=f"raw_{w}") for w in ("w1", "w2", "wd")}
        raw["old"] = sb("old", [P, PACK, S], F32)
        old = raw["old"]
        unit_t = sb("unit_t", [P, PACK], F32)
        fade_rows = sb("fade_rows", [P, P], F32)
        ident = sb("ident", [P, P], F32)

        def load_weight(w):
            nc.sync.dma_start(out=raw[w][:], in_=weights[w].rearrange("(p j) n -> p j n", j=PACK))

        def load_mem(t):
            nc.sync.dma_start(out=mem_t[t][:], in_=mem.rearrange("(p t) u -> p t u", t=PACK)[:, t, :])

        nc.gpsimd.memset(xs_table[:].bitcast(I32), 0)
        nc.sync.dma_start(out=x_table[:], in_=x_words[0].rearrange("p n t -> p (n t)").bitcast(I32))
        for q in range(QUADS):
            nc.sync.dma_start(
                out=xs_table[32 * q : 32 * q + 4, :].bitcast(I32),
                in_=x_scales[0, 4 * q : 4 * q + 4, :].bitcast(I32),
            )
        nc.sync.dma_start(offs_t[:], offs)
        nc.sync.dma_start(out=fade_rows[:], in_=fade.rearrange("r (c m) -> (r c) m", m=P)[0:P, :])
        load_weight("w1")
        nc.sync.dma_start(slot_t[:], slot)
        load_weight("w2")
        load_mem(0)
        load_mem(1)
        load_mem(2)
        load_mem(3)
        nc.sync.dma_start(out=unit_t[:], in_=unit.rearrange("(p t) o -> p (t o)", t=PACK))
        w3_view = w3.rearrange("(p j) n -> p j n", j=PACK)
        raw_w3a = sb("raw_w3a", [P, PACK, 256], F32, tag="raw_w3a")
        raw_w3b = sb("raw_w3b", [P, PACK, N - 256], F32)
        nc.sync.dma_start(out=raw_w3a[:], in_=w3_view[:, :, 0:256])
        nc.sync.dma_start(out=raw_w3b[:], in_=w3_view[:, :, 256:N])
        load_weight("wd")
        make_identity(nc, ident[:])
        warm = sb("warm", [P, 2], F32)
        nc.vector.memset(warm[:, 0:1], 0.0)
        nc.scalar.activation(out=warm[:, 1:2], in_=warm[:, 0:1], func=ACT.Sigmoid)

        def interleave(engine, dst, src):
            d = dst.rearrange("p (c i) t -> p c t i", i=4)
            s = src.rearrange("p t (c i) -> p c t i", i=4)
            if engine == "scalar":
                nc.scalar.copy(out=d, in_=s)
            elif engine == "gpsimd":
                nc.gpsimd.tensor_scalar(out=d, in0=s, scalar1=1.0, scalar2=0.0, op0=ALU.mult, op1=ALU.add)
            else:
                nc.vector.tensor_copy(out=d, in_=s)

        def quantize(codes_ap, scales_ap, grouped_ap):
            nc.vector.quantize_mx(
                out=codes_ap.bitcast(FP8X4), scales=scales_ap, in_=grouped_ap.rearrange("p c t -> p (c t)")
            )

        kept = sb("kept", [P, PACK, S], F32)
        grouped = {w: sb(f"grp_{w}", [P, N, PACK], BF16) for w in weights}
        grouped["old"] = sb("grp_old", [P, S, PACK], BF16, tag="raw_w3a")
        codes = {name: sb(f"codes_{name}", [P, N], U32) for name in list(weights) + ["old", "x"]}
        scales = {name: sb(f"scales_{name}", [P, N], U8) for name in list(weights) + ["old", "x"]}

        def round_columns(name, first, last, engine):
            cols = slice(first, last)
            interleave(engine, grouped[name][:, cols, :], raw[name][:, :, cols])

        def quantize_operand(name):
            quantize(codes[name][:], scales[name][:], grouped[name][:])

        partner = {"w1": "x", "w2": "x", "w3": "x", "wd": "old"}
        func = {"w1": ACT.Sigmoid, "w2": ACT.Sigmoid, "w3": ACT.Tanh, "wd": ACT.Tanh}
        first_bank = {"w1": 0, "w2": 4, "w3": 0, "wd": 4}
        gate_tiles = {w: sb(f"gate_{w}", [P, CHUNKS, PACK, P], F32, tag="" if w == "w1" else "") for w in weights}
        gates = {(w, c): gate_tiles[w][:, c] for w in weights for c in range(CHUNKS)}

        def gate(w, c):
            cols = slice(c * P, (c + 1) * P)
            bank = banks[first_bank[w] + c]
            nc.tensor.matmul_mx(
                out=bank[:],
                lhsT=codes[partner[w]][:, cols].bitcast(FP8X4),
                lhsT_scale=scales[partner[w]][:, cols],
                rhs=codes[w][:].bitcast(FP8X4),
                rhs_scale=scales[w][:],
                start=True,
                stop=True,
            )
            nc.scalar.activation(out=gates[w, c][:], in_=bank[:].rearrange("p (m t) -> p t m", t=PACK), func=func[w])

        def gather_mem(t):
            nc.vector.tensor_copy(old[:, t, :], mem_t[t][:].indirect(slot_t[:]))

        fade_m1 = sb("fade_m1", [P, CHUNKS], F32)
        f_banks = {}
        sums = {}
        new_all = sb("new", [P, CHUNKS, PACK, P], F32, tag="raw_wd")

        def fade_column():
            fade_ps = banks[4]
            nc.tensor.transpose(fade_ps[:, 0:P], fade_rows[:], ident[:])
            nc.vector.tensor_scalar_add(fade_m1[:], fade_ps[:, 0:CHUNKS], -1.0)

        def turn_forget(t):
            f_banks[t] = banks[4 + t][:].rearrange("p (c m) -> p c m", c=CHUNKS)
            for c in range(CHUNKS):
                nc.tensor.transpose(f_banks[t][:, c, :], gates["w1", c][:, t, :], ident[:])

        def kept_term(t):
            nc.vector.scalar_tensor_tensor(
                out=kept[:, t, :],
                in0=old[:, t, :],
                scalar=unit_t[:, t : t + 1],
                in1=f_banks[t][:].rearrange("p c m -> p (c m)"),
                op0=ALU.mult,
                op1=ALU.mult,
            )

        def new_term(c, engine):
            new = new_all[:, c]
            engine.tensor_tensor(out=new[:], in0=gates["w2", c][:], in1=gates["w3", c][:], op=ALU.mult)
            sums[c] = banks[0 + c][:].rearrange("p (t m) -> p t m", t=PACK)
            for t in range(PACK):
                nc.tensor.matmul(
                    sums[c][:, t, :], lhsT=new[:, t, :], rhs=ident[:], is_transpose=True, start=(t == 0), stop=False
                )

        def lost_term(c):
            lost = sb(f"lost{c}", [P, PACK, P], F32)
            nc.vector.scalar_tensor_tensor(
                out=lost[:],
                in0=gates["wd", c][:],
                scalar=fade_m1[:, c : c + 1],
                in1=gates["w1", c][:],
                op0=ALU.mult,
                op1=ALU.mult,
            )
            for t in range(PACK):
                nc.tensor.matmul(
                    sums[c][:, t, :], lhsT=lost[:, t, :], rhs=ident[:], is_transpose=True, start=False, stop=(t == PACK - 1)
                )

        y_codes = sb("y_codes", [P, S], U32)
        y_scales = sb("y_scales", [P, S], U8)
        out_rows = out_0.rearrange("(p t) n -> p t n", t=PACK)
        out_words = out_1[0].rearrange("p n t -> p (n t)").bitcast(I32)
        y_grouped = {}

        def result(c, engine):
            cols = slice(c * P, (c + 1) * P)
            y = sb(f"y{c}", [P, PACK, P], F32)
            nc.vector.tensor_tensor(out=y[:], in0=kept[:, :, cols], in1=sums[c][:], op=ALU.add)
            nc.sync.dma_start(out=out_rows[:, :, cols], in_=y[:])
            y_grouped[c] = sb(f"y_grouped{c}", [P, P, PACK], BF16)
            interleave(engine, y_grouped[c][:], y[:])

        def planes(c):
            cols = slice(c * P, (c + 1) * P)
            quantize(y_codes[:, cols], y_scales[:, cols], y_grouped[c][:])
            if c % 2 == 1:
                done = slice((c - 1) * P, (c + 1) * P)
                nc.sync.dma_start(out=out_words[:, done], in_=y_codes[:, done].bitcast(I32))

        nc.vector.tensor_copy(codes["x"][:], x_table[:].bitcast(U32).indirect(offs_t[:]))
        nc.vector.tensor_copy(scales["x"][:], xs_table[:].indirect(offs_t[:]))
        fade_column()
        round_columns("w1", 0, 192, "scalar")
        round_columns("w1", 192, 512, "vector")
        quantize_operand("w1")
        round_columns("w2", 0, 512, "vector")
        quantize_operand("w2")
        gate("w1", 0)
        gate("w1", 1)
        gate("w1", 2)
        gate("w1", 3)
        gather_mem(0)
        gather_mem(1)
        gate("w2", 0)
        gate("w2", 1)
        gate("w2", 2)
        gate("w2", 3)
        turn_forget(0)
        turn_forget(1)
        turn_forget(2)
        turn_forget(3)
        gather_mem(2)
        gather_mem(3)
        interleave("scalar", grouped["w3"][:, 0:256, :], raw_w3a[:])
        interleave("scalar", grouped["w3"][:, 256:N, :], raw_w3b[:])
        round_columns("old", 0, 256, "scalar")
        round_columns("old", 256, 512, "scalar")
        quantize_operand("w3")
        round_columns("wd", 0, 128, "scalar")
        round_columns("wd", 128, 512, "vector")
        quantize_operand("wd")
        quantize_operand("old")
        kept_term(0)
        kept_term(1)
        kept_term(2)
        kept_term(3)
        gate("w3", 0)
        gate("w3", 1)
        gate("w3", 2)
        gate("w3", 3)
        gate("wd", 0)
        gate("wd", 1)
        gate("wd", 2)
        gate("wd", 3)
        new_term(0, nc.vector)
        new_term(1, nc.vector)
        new_term(2, nc.vector)
        new_term(3, nc.vector)
        lost_term(0)
        lost_term(1)
        lost_term(2)
        result(0, "scalar")
        lost_term(3)
        result(1, "scalar")
        planes(0)
        result(2, "scalar")
        planes(1)
        result(3, "vector")
        planes(2)
        planes(3)
        for q in range(QUADS):
            queue = nc.sync if q % 2 == 0 else nc.scalar
            queue.dma_start(
                out=out_2[0, 4 * q : 4 * q + 4, :].bitcast(I32),
                in_=y_scales[32 * q : 32 * q + 4, :].bitcast(I32),
            )
